import numpy as np, ml_dtypes
CORES = [65,66,69,71,193,194,197,199,321,322,325,327,449,450,453,455]
N = 16
WB, KB, QP = 2, 1, 128
def setup_inputs(rng):
    return {"q": rng.standard_normal((N, 128, QP), dtype=np.float32).astype(ml_dtypes.bfloat16), "k": rng.standard_normal((N, 128, KB * 128), dtype=np.float32).astype(ml_dtypes.bfloat16), "v": rng.standard_normal((N, 128, KB * 128), dtype=np.float32).astype(ml_dtypes.bfloat16)}
def setup_inputs_big(rng):
    d = setup_inputs(rng)
    for k in ("q", "k", "v"): d[k] = (d[k].astype(np.float32) * 1024.0).astype(d[k].dtype)
    return d
def setup_inputs_small(rng):
    d = setup_inputs(rng)
    for k in ("q", "k", "v"): d[k] = (d[k].astype(np.float32) * (1 / 1024.0)).astype(d[k].dtype)
    return d
def setup_inputs_apart(rng):
    d = setup_inputs(rng)
    f = (10.0 ** rng.permutation(np.linspace(-1.5, 1.5, N))).astype(np.float32).reshape(N, 1, 1)
    for k in ("q", "k", "v"): d[k] = (d[k].astype(np.float32) * f).astype(d[k].dtype)
    return d
def reference(q, k, v):
    Q, K, V = q.astype(np.float64), k.astype(np.float64), v.astype(np.float64)
    y = np.zeros((N, 128, QP))
    for r in range(N):
        for j in range(max(0, r - WB), r + 1):
            for b in range(KB):
                S = np.maximum(K[j][:, 128 * b:128 * b + 128].T @ Q[r], 0.0)
                y[r] += V[j][:, 128 * b:128 * b + 128].T @ S
    return {"y": y.astype(ml_dtypes.bfloat16 if q.dtype != np.float64 else np.float64)}

@@ -1,0 +1,122 @@
+from concourse.bass import DstId, RemoteDMATransfer
+from concourse.mybir import AluOpType
+
+P = 128
+WB = 2
+
+SCRATCH = {
+    "kv0": ("sbuf", [P, 2 * P], "bfloat16"),
+    "kv1": ("sbuf", [P, 2 * P], "bfloat16"),
+    "kv2": ("sbuf", [P, 2 * P], "bfloat16"),
+    "qs": ("sbuf", [P, P], "bfloat16"),
+    "zero": ("sbuf", [P, P], "float32"),
+    "s0": ("sbuf", [P, P], "bfloat16"),
+    "s1": ("sbuf", [P, P], "bfloat16"),
+    "s2": ("sbuf", [P, P], "bfloat16"),
+    "ys": ("sbuf", [P, P], "bfloat16"),
+    "ps0": ("psum", [P, 512], "float32"),
+    "ps1": ("psum", [P, 512], "float32"),
+    "ps2": ("psum", [P, 512], "float32"),
+    "po": ("psum", [P, 512], "float32"),
+}
+SEMAPHORES = ["ld", "ldq", "sent", "arr1", "arr2", "z", "ms0", "ms1", "ms2", "rl0", "rl1", "rl2", "mo", "cp", "st"]
+
+
+def _engines(mask):
+    return [e for e in range(mask.bit_length()) if (mask >> e) & 1]
+
+
+def _bits(es):
+    m = 0
+    for e in es:
+        m |= 1 << e
+    return m
+
+
+def _same_chip(topo, a, b):
+    return (topo.host(a), topo.chip(a)) == (topo.host(b), topo.chip(b))
+
+
+def _plan(cores, topo, j):
+    src = cores[j]
+    dests = [(d, cores[j + d]) for d in range(1, WB + 1) if j + d < len(cores)]
+    off = [(d, c) for d, c in dests if not _same_chip(topo, src, c)]
+    on = [(d, c) for d, c in dests if _same_chip(topo, src, c)]
+    calls = []
+    if len(off) == 2 or len(on) == 2:
+        two = off if off else on
+        es = _engines(topo.mask(src, two[0][1]) & topo.mask(src, two[1][1]))
+        es = es[:8]
+        h = len(es) // 2
+        calls.append([(two[0][0], two[0][1], _bits(es[:h])), (two[1][0], two[1][1], _bits(es[h:]))])
+    else:
+        used = 0
+        for d, c in off + on:
+            es = _engines(topo.mask(src, c) & ~used)[:8]
+            calls.append([(d, c, _bits(es))])
+            used |= _bits(es)
+    return calls
+
+
+def _count(cores, topo, j, d):
+    for call in _plan(cores, topo, j):
+        for dd, _c, m in call:
+            if dd == d:
+                return len(_engines(m))
+    return 0
+
+
+def rank_program(g, core, T, topo):
+    r = T.rank_of(core)
+    if r is None:
+        return
+    cores = list(T.cores)
+    S = T.sem
+    te, ve = g.tensor, g.vector
+
+    g.sync.dma_start(T.kv0[:, 0:P], T.k[:]).then_inc(S.ld, 16)
+    g.scalar.dma_start(T.kv0[:, P:2 * P], T.v[:]).then_inc(S.ld, 16)
+    g.sync.dma_start(T.qs[:], T.q[:]).then_inc(S.ldq, 16)
+
+    calls = _plan(cores, topo, r)
+    if calls:
+        g.wait_ge(S.ld, 32)
+        total = 0
+        for call in calls:
+            trs = []
+            for d, c, m in call:
+                rid, pid = topo.addr(c, core)
+                trs.append(RemoteDMATransfer(dst_ids=[DstId(rid=rid, pnc=pid)], dma_engine_mask=m,
+                                             remote_sem=S["arr%d" % d], src=T.kv0[:], dst=T["kv%d" % d][:]))
+                total += len(_engines(m))
+            g.remote_dma_fused(trs, local_sem=S.sent)
+        g.wait_ge(S.sent, total)
+
+    back = [d for d in range(1, WB + 1) if r - d >= 0]
+    back.sort(key=lambda d: (0 if _same_chip(topo, cores[r - d], core) else 1, -d))
+    n = 1 + len(back)
+
+    te.wait_ge(S.ld, 32)
+    te.wait_ge(S.ldq, 16)
+    te.matmul(T.ps0[:, 0:P], T.kv0[:, 0:P], T.qs[:], True, True).then_inc(S.ms0, 1)
+    te.wait_ge(S.rl0, 1)
+    mm = te.matmul(T.po[:, 0:P], T.kv0[:, P:2 * P], T.s0[:], True, n == 1)
+    for d in back:
+        te.wait_ge(S["arr%d" % d], _count(cores, topo, r - d, d))
+        te.matmul(T["ps%d" % d][:, 0:P], T["kv%d" % d][:, 0:P], T.qs[:], True, True).then_inc(S["ms%d" % d], 1)
+    for i, d in enumerate(back):
+        te.wait_ge(S["rl%d" % d], 1)
+        mm = te.matmul(T.po[:, 0:P], T["kv%d" % d][:, P:2 * P], T["s%d" % d][:], False, i == len(back) - 1)
+    mm.then_inc(S.mo, 1)
+
+    ve.memset(T.zero[:], 0.0).then_inc(S.z, 1)
+    ve.wait_ge(S.z, 1)
+    for d in [0] + back:
+        ve.wait_ge(S["ms%d" % d], 1)
+        ve.tensor_tensor(T["s%d" % d][:], T["ps%d" % d][:, 0:P], T.zero[:], AluOpType.max).then_inc(S["rl%d" % d], 1)
+    ve.wait_ge(S.mo, 1)
+    ve.tensor_copy(T.ys[:], T.po[:, 0:P]).then_inc(S.cp, 1)
+
+    g.sync.wait_ge(S.cp, 1)
+    g.sync.dma_start(T.y[:], T.ys[:]).then_inc(S.st, 16)
+    g.sync.wait_ge(S.st, 16)

@@ -3,6 +3,8 @@ from concourse.mybir import AluOpType
 
 P = 128
 WB = 2
+E_TWO = 8
+E_ONE = 8
 
 SCRATCH = {
     "kv0": ("sbuf", [P, 2 * P], "bfloat16"),
@@ -19,7 +21,8 @@ SCRATCH = {
     "ps2": ("psum", [P, 512], "float32"),
     "po": ("psum", [P, 512], "float32"),
 }
-SEMAPHORES = ["ld", "ldq", "sent", "arr1", "arr2", "z", "ms0", "ms1", "ms2", "rl0", "rl1", "rl2", "mo", "cp", "st"]
+SEMAPHORES = ["ld", "ldq", "sent", "arr1", "arr2", "x1", "x2", "z", "ms0", "ms1", "ms2", "rl0", "rl1", "rl2", "mo", "cp",
+              "st"]
 
 
 def _engines(mask):
@@ -37,6 +40,13 @@ def _same_chip(topo, a, b):
     return (topo.host(a), topo.chip(a)) == (topo.host(b), topo.chip(b))
 
 
+def _split(cores, topo, j):
+    if j < 0 or j + WB >= len(cores):
+        return False
+    a, b = cores[j + 1], cores[j + 2]
+    return _same_chip(topo, a, b) and not _same_chip(topo, cores[j], a)
+
+
 def _plan(cores, topo, j):
     src = cores[j]
     dests = [(d, cores[j + d]) for d in range(1, WB + 1) if j + d < len(cores)]
@@ -45,24 +55,27 @@ def _plan(cores, topo, j):
     calls = []
     if len(off) == 2 or len(on) == 2:
         two = off if off else on
-        es = _engines(topo.mask(src, two[0][1]) & topo.mask(src, two[1][1]))
-        es = es[:8]
+        es = _engines(topo.mask(src, two[0][1]) & topo.mask(src, two[1][1]))[:E_TWO]
         h = len(es) // 2
-        calls.append([(two[0][0], two[0][1], _bits(es[:h])), (two[1][0], two[1][1], _bits(es[h:]))])
+        if _split(cores, topo, j):
+            cols = [(0, P), (P, 2 * P)]
+        else:
+            cols = [(0, 2 * P), (0, 2 * P)]
+        calls.append([(two[0][0], two[0][1], _bits(es[:h])) + cols[0], (two[1][0], two[1][1], _bits(es[h:])) + cols[1]])
     else:
         used = 0
         for d, c in off + on:
-            es = _engines(topo.mask(src, c) & ~used)[:8]
-            calls.append([(d, c, _bits(es))])
+            es = _engines(topo.mask(src, c) & ~used)[:E_ONE]
+            calls.append([(d, c, _bits(es), 0, 2 * P)])
             used |= _bits(es)
     return calls
 
 
 def _count(cores, topo, j, d):
     for call in _plan(cores, topo, j):
-        for dd, _c, m in call:
-            if dd == d:
-                return len(_engines(m))
+        for t in call:
+            if t[0] == d:
+                return len(_engines(t[2]))
     return 0
 
 
@@ -78,23 +91,43 @@ def rank_program(g, core, T, topo):
     g.scalar.dma_start(T.kv0[:, P:2 * P], T.v[:]).then_inc(S.ld, 16)
     g.sync.dma_start(T.qs[:], T.q[:]).then_inc(S.ldq, 16)
 
+    total = 0
     calls = _plan(cores, topo, r)
     if calls:
         g.wait_ge(S.ld, 32)
-        total = 0
         for call in calls:
             trs = []
-            for d, c, m in call:
+            for d, c, m, c0, c1 in call:
                 rid, pid = topo.addr(c, core)
                 trs.append(RemoteDMATransfer(dst_ids=[DstId(rid=rid, pnc=pid)], dma_engine_mask=m,
-                                             remote_sem=S["arr%d" % d], src=T.kv0[:], dst=T["kv%d" % d][:]))
+                                             remote_sem=S["arr%d" % d], src=T.kv0[:, c0:c1], dst=T["kv%d" % d][:, c0:c1]))
                 total += len(_engines(m))
             g.remote_dma_fused(trs, local_sem=S.sent)
+
+    XE = {}
+    for d in range(1, WB + 1):
+        if _split(cores, topo, r - d):
+            peer, pd = (cores[r + 1], 2) if d == 1 else (cores[r - 1], 1)
+            c0 = 0 if d == 1 else P
+            m = _bits(_engines(topo.mask(core, peer))[:E_ONE])
+            XE[d] = len(_engines(_bits(_engines(topo.mask(peer, core))[:E_ONE])))
+            rid, pid = topo.addr(peer, core)
+            g.wait_ge(S["arr%d" % d], _count(cores, topo, r - d, d))
+            g.remote_dma(T["kv%d" % pd][:, c0:c0 + P], T["kv%d" % d][:, c0:c0 + P], S["x%d" % pd], S.sent, pid, rid, m)
+            total += len(_engines(m))
+    if total:
         g.wait_ge(S.sent, total)
 
     back = [d for d in range(1, WB + 1) if r - d >= 0]
     back.sort(key=lambda d: (0 if _same_chip(topo, cores[r - d], core) else 1, -d))
     n = 1 + len(back)
+
+    def waits(d):
+        direct = (S["arr%d" % d], _count(cores, topo, r - d, d))
+        if d not in XE:
+            return direct, direct
+        passed = (S["x%d" % d], XE[d])
+        return (direct, passed) if d == 1 else (passed, direct)
 
     te.wait_ge(S.ld, 32)
     te.wait_ge(S.ldq, 16)
@@ -102,9 +135,10 @@ def rank_program(g, core, T, topo):
     te.wait_ge(S.rl0, 1)
     mm = te.matmul(T.po[:, 0:P], T.kv0[:, P:2 * P], T.s0[:], True, n == 1)
     for d in back:
-        te.wait_ge(S["arr%d" % d], _count(cores, topo, r - d, d))
+        te.wait_ge(*waits(d)[0])
         te.matmul(T["ps%d" % d][:, 0:P], T["kv%d" % d][:, 0:P], T.qs[:], True, True).then_inc(S["ms%d" % d], 1)
     for i, d in enumerate(back):
+        te.wait_ge(*waits(d)[1])
         te.wait_ge(S["rl%d" % d], 1)
         mm = te.matmul(T.po[:, 0:P], T["kv%d" % d][:, P:2 * P], T["s%d" % d][:], False, i == len(back) - 1)
     mm.then_inc(S.mo, 1)

@@ -3,13 +3,13 @@ from concourse.mybir import AluOpType
 
 P = 128
 WB = 2
-E_TWO = 8
-E_ONE = 8
+NE = 8
 
 SCRATCH = {
     "kv0": ("sbuf", [P, 2 * P], "bfloat16"),
     "kv1": ("sbuf", [P, 2 * P], "bfloat16"),
     "kv2": ("sbuf", [P, 2 * P], "bfloat16"),
+    "rv": ("sbuf", [P, P], "bfloat16"),
     "qs": ("sbuf", [P, P], "bfloat16"),
     "zero": ("sbuf", [P, P], "float32"),
     "s0": ("sbuf", [P, P], "bfloat16"),
@@ -21,7 +21,7 @@ SCRATCH = {
     "ps2": ("psum", [P, 512], "float32"),
     "po": ("psum", [P, 512], "float32"),
 }
-SEMAPHORES = ["ld", "ldq", "sent", "arr1", "arr2", "x1", "x2", "z", "ms0", "ms1", "ms2", "rl0", "rl1", "rl2", "mo", "cp",
+SEMAPHORES = ["ld", "ldq", "sent", "k1", "v1", "k2", "v2", "rvs", "z", "ms0", "ms1", "ms2", "rl0", "rl1", "rl2", "mo", "cp",
               "st"]
 
 
@@ -40,43 +40,65 @@ def _same_chip(topo, a, b):
     return (topo.host(a), topo.chip(a)) == (topo.host(b), topo.chip(b))
 
 
-def _split(cores, topo, j):
-    if j < 0 or j + WB >= len(cores):
-        return False
-    a, b = cores[j + 1], cores[j + 2]
-    return _same_chip(topo, a, b) and not _same_chip(topo, cores[j], a)
+def _dests(cores, j):
+    return [(d, cores[j + d]) for d in range(1, WB + 1) if j + d < len(cores)]
 
 
-def _plan(cores, topo, j):
+def _leaves(cores, topo, j):
+    return [(d, c) for d, c in _dests(cores, j) if not _same_chip(topo, cores[j], c)]
+
+
+def _carriers(cores, topo, j):
     src = cores[j]
-    dests = [(d, cores[j + d]) for d in range(1, WB + 1) if j + d < len(cores)]
-    off = [(d, c) for d, c in dests if not _same_chip(topo, src, c)]
-    on = [(d, c) for d, c in dests if _same_chip(topo, src, c)]
-    calls = []
-    if len(off) == 2 or len(on) == 2:
-        two = off if off else on
-        es = _engines(topo.mask(src, two[0][1]) & topo.mask(src, two[1][1]))[:E_TWO]
-        h = len(es) // 2
-        if _split(cores, topo, j):
-            cols = [(0, P), (P, 2 * P)]
-        else:
-            cols = [(0, 2 * P), (0, 2 * P)]
-        calls.append([(two[0][0], two[0][1], _bits(es[:h])) + cols[0], (two[1][0], two[1][1], _bits(es[h:])) + cols[1]])
-    else:
+    return [c for i, c in enumerate(cores) if _same_chip(topo, c, src) and topo.die(c) != topo.die(src)
+            and not _leaves(cores, topo, i)]
+
+
+def _build(cores, topo):
+    calls = dict((c, [[], [], []]) for c in cores)
+    land = {}
+    for j, src in enumerate(cores):
+        off = _leaves(cores, topo, j)
+        on = [t for t in _dests(cores, j) if t not in off]
         used = 0
-        for d, c in off + on:
-            es = _engines(topo.mask(src, c) & ~used)[:E_ONE]
-            calls.append([(d, c, _bits(es), 0, 2 * P)])
-            used |= _bits(es)
-    return calls
-
-
-def _count(cores, topo, j, d):
-    for call in _plan(cores, topo, j):
-        for t in call:
-            if t[0] == d:
-                return len(_engines(t[2]))
-    return 0
+        if len(off) == 2:
+            (d1, c1), (d2, c2) = off
+            out = topo.mask(src, c1)
+            ek = _engines(out)[:NE // 2]
+            trs = [(c1, "kv0", 0, P, "kv%d" % d1, 0, P, "k%d" % d1, _bits(ek))]
+            land[(j + d1, d1, "k")] = ("k%d" % d1, len(ek))
+            car = _carriers(cores, topo, j)
+            ev = _engines(topo.mask(src, car[0]) & topo.mask(src, car[1]) & ~out)[:NE]
+            h = len(ev) // 2
+            for n, (d, c) in enumerate(off):
+                trs.append((car[n], "kv0", P, 2 * P, "rv", 0, P, "rvs", _bits(ev[n * h:(n + 1) * h])))
+                er = _engines(topo.mask(car[n], c))[:NE]
+                calls[car[n]][1].append((("rvs", h), [(c, "rv", 0, P, "kv%d" % d, P, 2 * P, "v%d" % d, _bits(er))]))
+                land[(j + d, d, "v")] = ("v%d" % d, len(er))
+            calls[src][0].append((None, trs))
+            ex = _engines(topo.mask(c1, c2))[:NE]
+            calls[c1][2].append((land[(j + d1, d1, "k")], [(c2, "kv%d" % d1, 0, P, "kv%d" % d2, 0, P, "k%d" % d2, _bits(ex))]))
+            land[(j + d2, d2, "k")] = ("k%d" % d2, len(ex))
+        elif off:
+            d, c = off[0]
+            es = _engines(topo.mask(src, c))[:NE]
+            used = _bits(es)
+            calls[src][0].append((None, [(c, "kv0", 0, P, "kv%d" % d, 0, P, "k%d" % d, used)]))
+            calls[src][0].append((None, [(c, "kv0", P, 2 * P, "kv%d" % d, P, 2 * P, "v%d" % d, used)]))
+            land[(j + d, d, "k")] = ("k%d" % d, len(es))
+            land[(j + d, d, "v")] = ("v%d" % d, len(es))
+        if on:
+            m = ~used
+            for _d, c in on:
+                m &= topo.mask(src, c)
+            es = _engines(m)[:NE]
+            h = len(es) // len(on)
+            trs = []
+            for n, (d, c) in enumerate(on):
+                trs.append((c, "kv0", 0, 2 * P, "kv%d" % d, 0, 2 * P, "k%d" % d, _bits(es[n * h:(n + 1) * h])))
+                land[(j + d, d, "k")] = land[(j + d, d, "v")] = ("k%d" % d, h)
+            calls[src][0].append((None, trs))
+    return calls, land
 
 
 def rank_program(g, core, T, topo):
@@ -86,35 +108,25 @@ def rank_program(g, core, T, topo):
     cores = list(T.cores)
     S = T.sem
     te, ve = g.tensor, g.vector
+    calls, land = _build(cores, topo)
 
     g.sync.dma_start(T.kv0[:, 0:P], T.k[:]).then_inc(S.ld, 16)
     g.scalar.dma_start(T.kv0[:, P:2 * P], T.v[:]).then_inc(S.ld, 16)
     g.sync.dma_start(T.qs[:], T.q[:]).then_inc(S.ldq, 16)
 
     total = 0
-    calls = _plan(cores, topo, r)
-    if calls:
-        g.wait_ge(S.ld, 32)
-        for call in calls:
-            trs = []
-            for d, c, m, c0, c1 in call:
+    g.wait_ge(S.ld, 32)
+    for stage in calls[core]:
+        for wait, trs in stage:
+            if wait is not None:
+                g.wait_ge(S[wait[0]], wait[1])
+            lst = []
+            for c, sb, s0, s1, db, d0, d1, sem, m in trs:
                 rid, pid = topo.addr(c, core)
-                trs.append(RemoteDMATransfer(dst_ids=[DstId(rid=rid, pnc=pid)], dma_engine_mask=m,
-                                             remote_sem=S["arr%d" % d], src=T.kv0[:, c0:c1], dst=T["kv%d" % d][:, c0:c1]))
+                lst.append(RemoteDMATransfer(dst_ids=[DstId(rid=rid, pnc=pid)], dma_engine_mask=m, remote_sem=S[sem],
+                                             src=T[sb][:, s0:s1], dst=T[db][:, d0:d1]))
                 total += len(_engines(m))
-            g.remote_dma_fused(trs, local_sem=S.sent)
-
-    XE = {}
-    for d in range(1, WB + 1):
-        if _split(cores, topo, r - d):
-            peer, pd = (cores[r + 1], 2) if d == 1 else (cores[r - 1], 1)
-            c0 = 0 if d == 1 else P
-            m = _bits(_engines(topo.mask(core, peer))[:E_ONE])
-            XE[d] = len(_engines(_bits(_engines(topo.mask(peer, core))[:E_ONE])))
-            rid, pid = topo.addr(peer, core)
-            g.wait_ge(S["arr%d" % d], _count(cores, topo, r - d, d))
-            g.remote_dma(T["kv%d" % pd][:, c0:c0 + P], T["kv%d" % d][:, c0:c0 + P], S["x%d" % pd], S.sent, pid, rid, m)
-            total += len(_engines(m))
+            g.remote_dma_fused(lst, local_sem=S.sent)
     if total:
         g.wait_ge(S.sent, total)
 
@@ -122,23 +134,18 @@ def rank_program(g, core, T, topo):
     back.sort(key=lambda d: (0 if _same_chip(topo, cores[r - d], core) else 1, -d))
     n = 1 + len(back)
 
-    def waits(d):
-        direct = (S["arr%d" % d], _count(cores, topo, r - d, d))
-        if d not in XE:
-            return direct, direct
-        passed = (S["x%d" % d], XE[d])
-        return (direct, passed) if d == 1 else (passed, direct)
-
     te.wait_ge(S.ld, 32)
     te.wait_ge(S.ldq, 16)
     te.matmul(T.ps0[:, 0:P], T.kv0[:, 0:P], T.qs[:], True, True).then_inc(S.ms0, 1)
     te.wait_ge(S.rl0, 1)
     mm = te.matmul(T.po[:, 0:P], T.kv0[:, P:2 * P], T.s0[:], True, n == 1)
     for d in back:
-        te.wait_ge(*waits(d)[0])
+        sem, cnt = land[(r, d, "k")]
+        te.wait_ge(S[sem], cnt)
         te.matmul(T["ps%d" % d][:, 0:P], T["kv%d" % d][:, 0:P], T.qs[:], True, True).then_inc(S["ms%d" % d], 1)
     for i, d in enumerate(back):
-        te.wait_ge(*waits(d)[1])
+        sem, cnt = land[(r, d, "v")]
+        te.wait_ge(S[sem], cnt)
         te.wait_ge(S["rl%d" % d], 1)
         mm = te.matmul(T.po[:, 0:P], T["kv%d" % d][:, P:2 * P], T["s%d" % d][:], False, i == len(back) - 1)
     mm.then_inc(S.mo, 1)

from concourse.bass import DstId, RemoteDMATransfer
from concourse.mybir import AluOpType

P = 128
WB = 2
NE = 8

SCRATCH = {
    "kv0": ("sbuf", [P, 2 * P], "bfloat16"),
    "kv1": ("sbuf", [P, 2 * P], "bfloat16"),
    "kv2": ("sbuf", [P, 2 * P], "bfloat16"),
    "rv": ("sbuf", [P, P], "bfloat16"),
    "qs": ("sbuf", [P, P], "bfloat16"),
    "zero": ("sbuf", [P, P], "float32"),
    "s0": ("sbuf", [P, P], "bfloat16"),
    "s1": ("sbuf", [P, P], "bfloat16"),
    "s2": ("sbuf", [P, P], "bfloat16"),
    "ys": ("sbuf", [P, P], "bfloat16"),
    "ps0": ("psum", [P, 512], "float32"),
    "ps1": ("psum", [P, 512], "float32"),
    "ps2": ("psum", [P, 512], "float32"),
    "po": ("psum", [P, 512], "float32"),
}
SEMAPHORES = ["ld", "ldq", "sent", "k1", "v1", "k2", "v2", "rvs", "z", "ms0", "ms1", "ms2", "rl0", "rl1", "rl2", "mo", "cp",
              "st"]


def _engines(mask):
    return [e for e in range(mask.bit_length()) if (mask >> e) & 1]


def _bits(es):
    m = 0
    for e in es:
        m |= 1 << e
    return m


def _same_chip(topo, a, b):
    return (topo.host(a), topo.chip(a)) == (topo.host(b), topo.chip(b))


def _dests(cores, j):
    return [(d, cores[j + d]) for d in range(1, WB + 1) if j + d < len(cores)]


def _leaves(cores, topo, j):
    return [(d, c) for d, c in _dests(cores, j) if not _same_chip(topo, cores[j], c)]


def _carriers(cores, topo, j):
    src = cores[j]
    return [c for i, c in enumerate(cores) if _same_chip(topo, c, src) and topo.die(c) != topo.die(src)
            and not _leaves(cores, topo, i)]


def _build(cores, topo):
    calls = dict((c, [[], [], []]) for c in cores)
    land = {}
    for j, src in enumerate(cores):
        off = _leaves(cores, topo, j)
        on = [t for t in _dests(cores, j) if t not in off]
        used = 0
        if len(off) == 2:
            (d1, c1), (d2, c2) = off
            out = topo.mask(src, c1)
            ek = _engines(out)[:NE // 2]
            trs = [(c1, "kv0", 0, P, "kv%d" % d1, 0, P, "k%d" % d1, _bits(ek))]
            land[(j + d1, d1, "k")] = ("k%d" % d1, len(ek))
            car = _carriers(cores, topo, j)
            ev = _engines(topo.mask(src, car[0]) & topo.mask(src, car[1]) & ~out)[:NE]
            h = len(ev) // 2
            for n, (d, c) in enumerate(off):
                trs.append((car[n], "kv0", P, 2 * P, "rv", 0, P, "rvs", _bits(ev[n * h:(n + 1) * h])))
                er = _engines(topo.mask(car[n], c))[:NE]
                calls[car[n]][1].append((("rvs", h), [(c, "rv", 0, P, "kv%d" % d, P, 2 * P, "v%d" % d, _bits(er))]))
                land[(j + d, d, "v")] = ("v%d" % d, len(er))
            calls[src][0].append((None, trs))
            ex = _engines(topo.mask(c1, c2))[:NE]
            calls[c1][2].append((land[(j + d1, d1, "k")], [(c2, "kv%d" % d1, 0, P, "kv%d" % d2, 0, P, "k%d" % d2, _bits(ex))]))
            land[(j + d2, d2, "k")] = ("k%d" % d2, len(ex))
        elif off:
            d, c = off[0]
            es = _engines(topo.mask(src, c))[:NE]
            used = _bits(es)
            calls[src][0].append((None, [(c, "kv0", 0, P, "kv%d" % d, 0, P, "k%d" % d, used)]))
            calls[src][0].append((None, [(c, "kv0", P, 2 * P, "kv%d" % d, P, 2 * P, "v%d" % d, used)]))
            land[(j + d, d, "k")] = ("k%d" % d, len(es))
            land[(j + d, d, "v")] = ("v%d" % d, len(es))
        if on:
            m = ~used
            for _d, c in on:
                m &= topo.mask(src, c)
            es = _engines(m)[:NE]
            h = len(es) // len(on)
            trs = []
            for n, (d, c) in enumerate(on):
                trs.append((c, "kv0", 0, 2 * P, "kv%d" % d, 0, 2 * P, "k%d" % d, _bits(es[n * h:(n + 1) * h])))
                land[(j + d, d, "k")] = land[(j + d, d, "v")] = ("k%d" % d, h)
            calls[src][0].append((None, trs))
    return calls, land


def rank_program(g, core, T, topo):
    r = T.rank_of(core)
    if r is None:
        return
    cores = list(T.cores)
    S = T.sem
    te, ve = g.tensor, g.vector
    calls, land = _build(cores, topo)

    g.sync.dma_start(T.kv0[:, 0:P], T.k[:]).then_inc(S.ld, 16)
    g.scalar.dma_start(T.kv0[:, P:2 * P], T.v[:]).then_inc(S.ld, 16)
    g.sync.dma_start(T.qs[:], T.q[:]).then_inc(S.ldq, 16)

    total = 0
    g.wait_ge(S.ld, 32)
    for stage in calls[core]:
        for wait, trs in stage:
            if wait is not None:
                g.wait_ge(S[wait[0]], wait[1])
            lst = []
            for c, sb, s0, s1, db, d0, d1, sem, m in trs:
                rid, pid = topo.addr(c, core)
                lst.append(RemoteDMATransfer(dst_ids=[DstId(rid=rid, pnc=pid)], dma_engine_mask=m, remote_sem=S[sem],
                                             src=T[sb][:, s0:s1], dst=T[db][:, d0:d1]))
                total += len(_engines(m))
            g.remote_dma_fused(lst, local_sem=S.sent)
    if total:
        g.wait_ge(S.sent, total)

    back = [d for d in range(1, WB + 1) if r - d >= 0]
    back.sort(key=lambda d: (0 if _same_chip(topo, cores[r - d], core) else 1, -d))
    n = 1 + len(back)

    te.wait_ge(S.ld, 32)
    te.wait_ge(S.ldq, 16)
    te.matmul(T.ps0[:, 0:P], T.kv0[:, 0:P], T.qs[:], True, True).then_inc(S.ms0, 1)
    te.wait_ge(S.rl0, 1)
    mm = te.matmul(T.po[:, 0:P], T.kv0[:, P:2 * P], T.s0[:], True, n == 1)
    for d in back:
        sem, cnt = land[(r, d, "k")]
        te.wait_ge(S[sem], cnt)
        te.matmul(T["ps%d" % d][:, 0:P], T["kv%d" % d][:, 0:P], T.qs[:], True, True).then_inc(S["ms%d" % d], 1)
    for i, d in enumerate(back):
        sem, cnt = land[(r, d, "v")]
        te.wait_ge(S[sem], cnt)
        te.wait_ge(S["rl%d" % d], 1)
        mm = te.matmul(T.po[:, 0:P], T["kv%d" % d][:, P:2 * P], T["s%d" % d][:], False, i == len(back) - 1)
    mm.then_inc(S.mo, 1)

    ve.memset(T.zero[:], 0.0).then_inc(S.z, 1)
    ve.wait_ge(S.z, 1)
    for d in [0] + back:
        ve.wait_ge(S["ms%d" % d], 1)
        ve.tensor_tensor(T["s%d" % d][:], T["ps%d" % d][:, 0:P], T.zero[:], AluOpType.max).then_inc(S["rl%d" % d], 1)
    ve.wait_ge(S.mo, 1)
    ve.tensor_copy(T.ys[:], T.po[:, 0:P]).then_inc(S.cp, 1)

    g.sync.wait_ge(S.cp, 1)
    g.sync.dma_start(T.y[:], T.ys[:]).then_inc(S.st, 16)
    g.sync.wait_ge(S.st, 16)
